import numpy as np
import ml_dtypes


def mxq(x, axis, fmt="e4m3"):
    dtype, down = {"e4m3": (ml_dtypes.float8_e4m3fn, 7), "e5m2": (ml_dtypes.float8_e5m2, 14)}[fmt]
    v = np.moveaxis(np.asarray(x, np.float32).astype(ml_dtypes.bfloat16).astype(np.float64), axis, -1)
    blocks = v.reshape(v.shape[:-1] + (-1, 32))
    amax = np.abs(blocks).max(-1, keepdims=True)
    byte = np.maximum(np.where(amax > 0, np.frexp(amax)[1] - 1 + 127, 0) - down, 1)
    scale = np.exp2(byte - 127.0)
    codes = (blocks / scale).astype(np.float32).astype(dtype).astype(np.float64)
    return np.moveaxis((codes * scale).reshape(v.shape), -1, axis)


WIDE = False


def mx_kscale(k):
    if not WIDE:
        return np.ones(k)
    levels = np.array([10, -10, 5, -5, 0])
    if k % 512:
        return np.exp2(np.random.permutation(np.resize(levels, k // 32))).repeat(32)
    a = np.empty((k // 512, 16))
    for p in range(k // 512):
        a[p, :8] = np.random.permutation(np.resize(levels, 8))
        for g in range(8):
            far = levels[np.abs(levels - a[p, g]) >= 10]
            a[p, g + 8] = far[np.random.randint(len(far))]
    return np.exp2(a.ravel()).repeat(32)


BF16 = ml_dtypes.bfloat16


def bf(x):
    return np.asarray(x, np.float32).astype(BF16)


def f64(x):
    return np.asarray(x).astype(np.float64)


E2M1 = np.array([0.0, 0.5, 1.0, 1.5, 2.0, 3.0, 4.0, 6.0, -0.0, -0.5, -1.0, -1.5, -2.0, -3.0, -4.0, -6.0])


def pack_weight(w, fmt):
    k, n = w.shape
    w = f64(bf(w)).reshape(k // 32, 32, n)
    amax = np.abs(w).max(1)
    if fmt == "e4m3":
        byte = np.frexp(amax)[1] - 1 + 127 - 7
    else:
        mant, ex = np.frexp(amax / 6.0)
        byte = np.where(mant > 0.5, ex, ex - 1) + 127
    byte = np.clip(np.where(amax > 0, byte, 1), 1, 254)
    scaled = (w * np.exp2(127.0 - byte)[:, None, :]).reshape(k, n).astype(np.float32)
    by_word = np.ascontiguousarray(scaled.reshape(k // 512, 128, 4, n).transpose(0, 1, 3, 2))
    if fmt == "e4m3":
        words = by_word.astype(ml_dtypes.float8_e4m3fn).view(np.uint8)
    else:
        c = by_word.astype(ml_dtypes.float4_e2m1fn).view(np.uint8) & 0xF
        words = c[..., 0::2] | (c[..., 1::2] << 4)
    return np.ascontiguousarray(words), np.ascontiguousarray(byte.astype(np.uint8).reshape(k // 512, 16, n))


def unpack_weight(words, scales, fmt):
    g, p, n, _ = words.shape
    if fmt == "e4m3":
        vals = np.ascontiguousarray(words).view(ml_dtypes.float8_e4m3fn).astype(np.float64)
    else:
        nib = np.empty((g, p, n, 4), np.uint8)
        nib[..., 0::2] = words & 0xF
        nib[..., 1::2] = words >> 4
        vals = E2M1[nib]
    vals = vals * np.repeat(np.exp2(scales.astype(np.float64) - 127.0), 8, axis=1)[..., None]
    return vals.transpose(0, 1, 3, 2).reshape(g * 512, n)
def pack4(w):
    words, scales = pack_weight(w, "e2m1")
    return words.reshape(words.shape[0], 128, -1), scales


def unpack4(words, scales):
    return unpack_weight(words.reshape(words.shape[0], 128, -1, 2), scales, "e2m1")


def planes(Y):
    n, m = Y.shape
    b = f64(bf(Y)).reshape(n // 32, 32, m)
    amax = np.abs(b).max(1)
    byte = np.clip(np.where(amax > 0, np.frexp(amax)[1] - 1 + 127 - 7, 1), 1, 254)
    codes = (b * np.exp2(127.0 - byte)[:, None, :]).reshape(n, m).astype(np.float32).astype(ml_dtypes.float8_e4m3fn).view(np.uint8)
    words = codes.reshape(n // 512, 128, 4, m).transpose(0, 1, 3, 2)
    return np.ascontiguousarray(words), np.ascontiguousarray(byte.astype(np.uint8).reshape(n // 512, 16, m))


SITES, R, NS, D = 4, 256, 1536, 1024


def setup_inputs():
    s = mx_kscale(SITES * D).reshape(SITES, D)
    t = mx_kscale(SITES * NS).reshape(SITES, NS)
    col = np.exp(0.7 * np.random.randn(SITES, D))
    x = np.random.randn(SITES, NS, D) * col[:, None, :] / np.sqrt(D)
    beta = 0.8 * np.random.randn(SITES, D)
    prob = 1.0 / (1.0 + np.exp(-(x * beta[:, None, :]).sum(axis=2)))
    weight = 2.0 * np.exp(0.3 * np.random.randn(SITES, NS))
    curv = weight * prob * (1.0 - prob)
    ridge = 0.5 * np.exp(0.8 * np.random.randn(SITES, D))
    v = np.random.randn(SITES, R, D)
    a_words, a_scales = pack4((x.swapaxes(1, 2) * s[:, :, None]).reshape(SITES * D, NS))
    b_words, b_scales = pack4((x / t[:, :, None]).reshape(SITES * NS, D))
    return {"v": bf(v / s[:, None, :]), "a_words": a_words, "a_scales": a_scales,
            "curv": bf(curv * t), "b_words": b_words, "b_scales": b_scales, "ridge": bf(ridge * s)}

def reference(v, a_words, a_scales, curv, b_words, b_scales, ridge):
    v, curv, ridge = f64(v), f64(curv), f64(ridge)
    a = unpack4(a_words, a_scales).reshape(SITES, D, NS)
    b = unpack4(b_words, b_scales).reshape(SITES, NS, D)
    h = (mxq(v, 2, "e4m3") @ a) * curv[:, None, :]
    y = (mxq(h, 2, "e4m3") @ b) + v * ridge[:, None, :]
    Y = y.reshape(SITES * R, D).T
    words, scales = planes(Y)
    return y, words, scales

@@ -1,0 +1,329 @@
+from contextlib import ExitStack
+
+import concourse.mybir as mybir
+from concourse.masks import make_identity
+
+SITES, R, NS, D = 4, 256, 1536, 1024
+FLOPS = 2 * 2 * SITES * R * NS * D
+
+F32 = mybir.dt.float32
+BF16 = mybir.dt.bfloat16
+I32 = mybir.dt.int32
+U32 = mybir.dt.uint32
+U8 = mybir.dt.uint8
+FP8X4 = mybir.dt.float8_e4m3fn_x4
+FP4X4 = mybir.dt.float4_e2m1fn_x4
+MULT = mybir.AluOpType.mult
+ADD = mybir.AluOpType.add
+
+P = 128
+KP = 512
+GD = D // KP
+GS = NS // KP
+UNITS = SITES * R // P
+PER_SITE = R // P
+BANKS = 8
+RIDGE_AHEAD = 3
+
+
+def tile_logistic_hessian_vector_sites_k7_kernel(
+    tc, v, a_words, a_scales, curv, b_words, b_scales, ridge, out_0, out_1, out_2
+):
+    nc = tc.nc
+    with ExitStack() as ctx:
+        keep = ctx.enter_context(tc.tile_pool(name="keep", bufs=1))
+        work = ctx.enter_context(tc.tile_pool(name="work", bufs=2))
+        psum = ctx.enter_context(tc.psum_pool(name="psum", bufs=1))
+
+        ident = keep.tile([P, P], F32, name="ident")
+        make_identity(nc, ident[:])
+        ctx.enter_context(tc.manual_schedule())
+
+        taken = []
+
+        def next_bank():
+            name = "bank%d" % (len(taken) % BANKS)
+            bank = psum.tile([P, KP], F32, name=name, tag=name)
+            taken.append(name)
+            return bank
+
+        def kept(name, shape, dtype):
+            tile = keep.tile(shape, dtype, name=name, tag=name, align_bytes=64)
+            return tile
+
+        def rotating(name, shape, dtype, bufs):
+            tile = work.tile(shape, dtype, name=name, tag=name, bufs=bufs, align_bytes=64)
+            return tile
+
+        a_scale, b_scale, a_parts, b_code, v_rows = {}, {}, {}, {}, {}
+        spread, v_tile = {}, {}
+        v_sorted, v_q, h_sorted, h_turned, h_q, v_ridge, y_rows, y_sorted = {}, {}, {}, {}, {}, {}, {}, {}
+        y_scale = kept("y_scale", [P, GD, SITES * R], U8)
+
+        def clear_scales(store, name, j, groups, width):
+            store[j] = kept("%s%d" % (name, j), [P, groups, width], U8)
+            nc.vector.memset(store[j][:].rearrange("p g n -> p (g n)").bitcast(I32), 0)
+
+        def load_scales(queue, store, dram, j, groups):
+            for r in range(4):
+                rows = dram[groups * j : groups * (j + 1), r:16:4, :].rearrange("g q n -> q g n")
+                queue.dma_start(out=store[j][r:P:32, :, :].bitcast(I32), in_=rows.bitcast(I32))
+
+        def load_a(j, n0, width):
+            part = kept("a%d_%d" % (j, n0), [P, GD, 2 * width], U8)
+            src = a_words[GD * j : GD * (j + 1), :, 2 * n0 : 2 * (n0 + width)].rearrange("g p n -> p g n")
+            nc.sync.dma_start(out=part[:].bitcast(I32), in_=src.bitcast(I32))
+            for n in range(n0, n0 + width, KP):
+                a_parts[j, n // KP] = (part, n - n0)
+
+        def load_b(j):
+            b_code[j] = kept("b%d" % j, [P, GS, 2 * D], U8)
+            src = b_words[GS * j : GS * (j + 1), :, :].rearrange("g p n -> p g n")
+            nc.sync.dma_start(out=b_code[j][:].bitcast(I32), in_=src.bitcast(I32))
+
+        def load_v(k, g0, groups):
+            j, h = divmod(k, PER_SITE)
+            tile = kept("v%d_%d" % (k, g0), [P, groups * KP], BF16)
+            nc.sync.dma_start(out=tile[:], in_=v[j, h * P : (h + 1) * P, g0 * KP : (g0 + groups) * KP])
+            for g in range(groups):
+                v_rows[k, g0 + g] = tile[:, g * KP : (g + 1) * KP]
+            v_tile[k] = tile
+
+        def load_spread(name, dram, j, g0, groups):
+            tile = kept("%s%d_%d" % (name, j, g0), [P, groups * KP], BF16)
+            nc.sync.dma_start(out=tile[:], in_=dram[j, g0 * KP : (g0 + groups) * KP].partition_broadcast(P))
+            for g in range(groups):
+                spread[name, j, g0 + g] = tile[:, g * KP : (g + 1) * KP]
+
+        def turn(words, count):
+            bank = next_bank()
+            for i in range(count):
+                nc.tensor.transpose(bank[:, i * P : (i + 1) * P], words[i], ident[:])
+            return bank
+
+        def word_blocks(tile, count):
+            words = tile[:].bitcast(F32)
+            return [words[:, i * P : (i + 1) * P] for i in range(count)]
+
+        def copy_turned(name, bank, groups, bufs):
+            tile = rotating(name, [P, groups * KP], BF16, bufs)
+            nc.scalar.copy(
+                out=tile[:].bitcast(F32).rearrange("p (g r u) -> p g r u", g=groups, u=2),
+                in_=bank[:, : groups * 2 * P].rearrange("p (g u r) -> p g r u", g=groups, u=2),
+            )
+            return tile
+
+        def quantize(name, tile, groups, bufs):
+            codes = rotating(name + "_codes", [P, groups * P], U32, bufs)
+            scales = rotating(name + "_scales", [P, groups * P], U8, bufs)
+            nc.vector.quantize_mx(out=codes[:].bitcast(FP8X4), scales=scales[:], in_=tile[:])
+            return [(codes[:, g * P : (g + 1) * P], scales[:, g * P : (g + 1) * P]) for g in range(groups)]
+
+        def sort_v(k):
+            v_sorted[k] = rotating("v_sorted", [P, D], BF16, 2)
+            nc.scalar.copy(
+                out=v_sorted[k][:].bitcast(F32).rearrange("r (g u p) -> r g u p", g=GD, u=2),
+                in_=v_tile[k][:].bitcast(F32).rearrange("r (g p u) -> r g u p", g=GD, u=2),
+            )
+
+        def stage_one(k, g):
+            j = k // PER_SITE
+            part, n0 = a_parts[j, g]
+            bank = next_bank()
+            for c in range(GD):
+                codes, scales = v_q[k][c]
+                nc.tensor.matmul_mx(
+                    out=bank[:],
+                    lhsT=codes.bitcast(FP8X4),
+                    lhsT_scale=scales,
+                    rhs=part[:, c, 2 * n0 : 2 * (n0 + KP)].bitcast(FP4X4),
+                    rhs_scale=a_scale[j][:, c, g * KP : (g + 1) * KP],
+                    start=(c == 0),
+                    stop=(c == GD - 1),
+                )
+            h_sorted[k, g] = rotating("h_sorted%d" % g, [P, KP], BF16, 2)
+            nc.vector.tensor_tensor(
+                out=h_sorted[k, g][:].rearrange("r (u p e) -> r u p e", u=2, e=2),
+                in0=bank[:].rearrange("r (p u e) -> r u p e", u=2, e=2),
+                in1=spread["curv", j, g].rearrange("r (p u e) -> r u p e", u=2, e=2),
+                op=MULT,
+            )
+
+        def ridge_term(k, c):
+            v_ridge[k, c] = rotating("v_ridge", [P, KP], F32, RIDGE_AHEAD)
+            nc.gpsimd.tensor_tensor(
+                out=v_ridge[k, c][:], in0=v_rows[k, c], in1=spread["ridge", k // PER_SITE, c], op=MULT
+            )
+
+        def stage_two(k, c):
+            j = k // PER_SITE
+            cols = slice(c * KP, (c + 1) * KP)
+            bank = next_bank()
+            for g in range(GS):
+                codes, scales = h_q[k][g]
+                nc.tensor.matmul_mx(
+                    out=bank[:],
+                    lhsT=codes.bitcast(FP8X4),
+                    lhsT_scale=scales,
+                    rhs=b_code[j][:, g, 2 * c * KP : 2 * (c + 1) * KP].bitcast(FP4X4),
+                    rhs_scale=b_scale[j][:, g, cols],
+                    start=(g == 0),
+                    stop=(g == GS - 1),
+                )
+            if c == 0:
+                y_rows[k] = kept("y%d" % k, [P, D], F32)
+            if (k, c) == (UNITS - 1, GD - 1):
+                y_sorted[k, c] = rotating("y_sorted%d" % c, [P, KP], BF16, 2)
+                nc.vector.tensor_tensor(
+                    out=y_sorted[k, c][:].rearrange("r (u p e) -> r u p e", u=2, e=2),
+                    in0=bank[:].rearrange("r (p u e) -> r u p e", u=2, e=2),
+                    in1=v_ridge[k, c][:].rearrange("r (p u e) -> r u p e", u=2, e=2),
+                    op=ADD,
+                )
+            nc.vector.tensor_tensor(out=y_rows[k][:, cols], in0=bank[:], in1=v_ridge[k, c][:], op=ADD)
+            ahead = GD * k + c + RIDGE_AHEAD
+            if ahead < GD * UNITS:
+                ridge_term(ahead // GD, ahead % GD)
+
+        def round_y(k, c):
+            y_sorted[k, c] = rotating("y_sorted%d" % c, [P, KP], BF16, 2)
+            nc.scalar.copy(
+                out=y_sorted[k, c][:].rearrange("r (u p e) -> r u p e", u=2, e=2),
+                in_=y_rows[k][:, c * KP : (c + 1) * KP].rearrange("r (p u e) -> r u p e", u=2, e=2),
+            )
+
+        def store_y(k, c0, count):
+            j, h = divmod(k, PER_SITE)
+            cols = slice(c0 * KP, (c0 + count) * KP)
+            nc.sync.dma_start(out=out_0[j, h * P : (h + 1) * P, cols], in_=y_rows[k][:, cols])
+
+        def turn_y(k, g0, groups):
+            blocks = []
+            for g in range(g0, g0 + groups):
+                blocks.extend(word_blocks(y_sorted[k, g], 2))
+            return turn(blocks, 2 * groups)
+
+        def planes(k, g0, groups, tile):
+            m = slice(k * P, (k + 1) * P)
+            codes = kept("y_codes%d_%d" % (k, g0), [P, groups, P], U32)
+            for g in range(groups):
+                nc.vector.quantize_mx(
+                    out=codes[:, g, :].bitcast(FP8X4),
+                    scales=y_scale[:, g0 + g, m],
+                    in_=tile[:, g * KP : (g + 1) * KP],
+                )
+            dst = out_1[g0 : g0 + groups, :, m, :].rearrange("g p m t -> p g (m t)")
+            nc.sync.dma_start(out=dst.bitcast(I32), in_=codes[:].bitcast(I32))
+
+        def load_site(j):
+            load_scales(nc.sync, a_scale, a_scales, j, GD)
+            load_a(j, 0, KP)
+            load_v(2 * j + 1, 0, GD)
+            load_a(j, KP, NS - KP)
+            load_spread("curv", curv, j, 0, GS)
+            load_spread("ridge", ridge, j, 0, GD)
+            load_scales(nc.sync, b_scale, b_scales, j, GS)
+            load_b(j)
+            if j + 1 < SITES:
+                load_v(2 * j + 2, 0, GD)
+
+        def stepped_blocks(rows):
+            words = rows.bitcast(F32)
+            return [words[:, u::2] for u in range(2)]
+
+        for j in range(SITES):
+            clear_scales(a_scale, "a_scale", j, GD, NS)
+            clear_scales(b_scale, "b_scale", j, GS, D)
+        load_v(0, 0, GD)
+        load_v(1, 0, GD)
+        load_scales(nc.sync, a_scale, a_scales, 0, GD)
+        load_a(0, 0, KP)
+        load_spread("curv", curv, 0, 0, 1)
+        load_a(0, KP, KP)
+        load_spread("ridge", ridge, 0, 0, GD)
+        load_a(0, 2 * KP, KP)
+        load_spread("curv", curv, 0, 1, GS - 1)
+        load_v(2, 0, GD)
+        load_scales(nc.sync, b_scale, b_scales, 0, GS)
+        load_b(0)
+        for j in range(1, SITES):
+            load_site(j)
+
+        v_q[0] = []
+        for g in range(GD):
+            bank_v = turn(stepped_blocks(v_rows[0, g]), 2)
+            v_q[0].extend(quantize("v_half", copy_turned("v_half_turned", bank_v, 1, 2), 1, 2))
+        bank_v = turn(stepped_blocks(v_rows[1, 0]) + stepped_blocks(v_rows[1, 1]), 4)
+        v_q[1] = quantize("v", copy_turned("v_turned", bank_v, GD, 2), GD, 2)
+        for g in range(GS):
+            stage_one(0, g)
+        for n in range(RIDGE_AHEAD):
+            ridge_term(n // GD, n % GD)
+
+        def turn_h(k):
+            bank_h = turn(word_blocks(h_sorted[k, 0], 2) + word_blocks(h_sorted[k, 1], 2), 4)
+            bank_last = turn(word_blocks(h_sorted[k, 2], 2), 2)
+            return bank_h, bank_last
+
+        def quantize_h(k, bank_h, bank_last):
+            h_q[k] = quantize("h", copy_turned("h_turned", bank_h, 2, 2), 2, 3)
+            h_q[k].extend(quantize("h_last", copy_turned("h_last_turned", bank_last, 1, 2), 1, 3))
+
+        for k in range(1, UNITS):
+            old = k - 2
+            if old >= 0:
+                stage_two(old, 0)
+                round_y(old, 0)
+                stage_two(old, 1)
+                round_y(old, 1)
+                store_y(old, 0, GD)
+            if k == 1:
+                sort_v(2)
+            for g in range(GS):
+                stage_one(k, g)
+            if old >= 1:
+                planes(old - 1, 0, GD, y_turned)
+
+            if k == 1:
+                banks_first = [turn(word_blocks(h_sorted[0, g], 2), 2) for g in range(GS)]
+            if k + 1 < UNITS:
+                bank_v = turn(word_blocks(v_sorted[k + 1], 4), 4)
+            if old >= 0:
+                bank_y = turn_y(old, 0, GD)
+            banks_h = turn_h(k)
+
+            if k == 1:
+                h_q[0] = []
+                for bank in banks_first:
+                    h_q[0].extend(quantize("h_first", copy_turned("h_first_turned", bank, 1, GS), 1, GS))
+            if k + 1 < UNITS:
+                v_q[k + 1] = quantize("v", copy_turned("v_turned", bank_v, GD, 2), GD, 2)
+            else:
+                planes(old, 0, GD, copy_turned("y_turned", bank_y, GD, 2))
+            quantize_h(k, *banks_h)
+            if 0 <= old < UNITS - 3:
+                y_turned = copy_turned("y_turned", bank_y, GD, 2)
+            if k + 2 < UNITS:
+                sort_v(k + 2)
+
+        old, last = UNITS - 2, UNITS - 1
+        stage_two(old, 0)
+        round_y(old, 0)
+        stage_two(old, 1)
+        round_y(old, 1)
+        store_y(old, 0, GD)
+        stage_two(last, 0)
+        round_y(last, 0)
+        store_y(last, 0, 1)
+        stage_two(last, 1)
+        bank_y = turn_y(old, 0, GD)
+        bank_first = turn_y(last, 0, 1)
+        bank_second = turn_y(last, 1, 1)
+        store_y(last, 1, 1)
+        planes(old, 0, GD, copy_turned("y_turned", bank_y, GD, 2))
+        planes(last, 0, 1, copy_turned("y_half_turned", bank_first, 1, 2))
+        planes(last, 1, 1, copy_turned("y_half_turned", bank_second, 1, 2))
+        for q in range(4):
+            queue = nc.scalar if q % 2 else nc.sync
+            dst = out_2[:, 4 * q : 4 * q + 4, :].rearrange("g q m -> q g m")
+            queue.dma_start(out=dst.bitcast(I32), in_=y_scale[32 * q : 32 * q + 4, :, :].bitcast(I32))

@@ -24,6 +24,8 @@ UNITS = SITES * R // P
 PER_SITE = R // P
 BANKS = 8
 RIDGE_AHEAD = 3
+CHUNK = 1024
+FIRST_ROW = {"curv": 0, "ridge": 32}
 
 
 def tile_logistic_hessian_vector_sites_k7_kernel(
@@ -57,6 +59,8 @@ def tile_logistic_hessian_vector_sites_k7_kernel(
 
         a_scale, b_scale, a_parts, b_code, v_rows = {}, {}, {}, {}, {}
         spread, v_tile = {}, {}
+        factor_rows = kept("factor_rows", [P, 2 * P], BF16)
+        columns = kept("columns", [P, 64], F32)
         v_sorted, v_q, h_sorted, h_turned, h_q, v_ridge, y_rows, y_sorted = {}, {}, {}, {}, {}, {}, {}, {}
         y_scale = kept("y_scale", [P, GD, SITES * R], U8)
 
@@ -89,11 +93,9 @@ def tile_logistic_hessian_vector_sites_k7_kernel(
                 v_rows[k, g0 + g] = tile[:, g * KP : (g + 1) * KP]
             v_tile[k] = tile
 
-        def load_spread(name, dram, j, g0, groups):
-            tile = kept("%s%d_%d" % (name, j, g0), [P, groups * KP], BF16)
-            nc.sync.dma_start(out=tile[:], in_=dram[j, g0 * KP : (g0 + groups) * KP].partition_broadcast(P))
-            for g in range(groups):
-                spread[name, j, g0 + g] = tile[:, g * KP : (g + 1) * KP]
+        def load_rows(dram, r0, count, p0):
+            flat = dram.rearrange("j n -> (j n)")[r0 * 2 * P : (r0 + count) * 2 * P]
+            nc.scalar.dma_start(out=factor_rows[p0 : p0 + count, :], in_=flat.rearrange("(r n) -> r n", n=2 * P))
 
         def turn(words, count):
             bank = next_bank()
@@ -104,6 +106,21 @@ def tile_logistic_hessian_vector_sites_k7_kernel(
         def word_blocks(tile, count):
             words = tile[:].bitcast(F32)
             return [words[:, i * P : (i + 1) * P] for i in range(count)]
+
+        def turn_columns(name, c):
+            first = FIRST_ROW[name] + 4 * c
+            return turn([columns[:, i : i + 1].to_broadcast([P, P]) for i in range(first, first + 4)], 4)
+
+        def copy_spread(name, c, bank):
+            spread[name, c] = kept("%s_spread%d" % (name, c), [P, CHUNK], BF16)
+            words = spread[name, c][:].bitcast(F32)
+            if name == "curv":
+                nc.scalar.copy(
+                    out=words.rearrange("m (g u p) -> m g u p", g=2, u=2),
+                    in_=bank[:].rearrange("m (g p u) -> m g u p", g=2, u=2),
+                )
+            else:
+                nc.scalar.copy(out=words, in_=bank[:])
 
         def copy_turned(name, bank, groups, bufs):
             tile = rotating(name, [P, groups * KP], BF16, bufs)
@@ -119,9 +136,9 @@ def tile_logistic_hessian_vector_sites_k7_kernel(
             nc.vector.quantize_mx(out=codes[:].bitcast(FP8X4), scales=scales[:], in_=tile[:])
             return [(codes[:, g * P : (g + 1) * P], scales[:, g * P : (g + 1) * P]) for g in range(groups)]
 
-        def sort_v(k):
+        def sort_v(k, copy):
             v_sorted[k] = rotating("v_sorted", [P, D], BF16, 2)
-            nc.scalar.copy(
+            copy(
                 out=v_sorted[k][:].bitcast(F32).rearrange("r (g u p) -> r g u p", g=GD, u=2),
                 in_=v_tile[k][:].bitcast(F32).rearrange("r (g p u) -> r g u p", g=GD, u=2),
             )
@@ -141,18 +158,19 @@ def tile_logistic_hessian_vector_sites_k7_kernel(
                     start=(c == 0),
                     stop=(c == GD - 1),
                 )
+            chunk, half = divmod(GS * j + g, 2)
             h_sorted[k, g] = rotating("h_sorted%d" % g, [P, KP], BF16, 2)
             nc.vector.tensor_tensor(
                 out=h_sorted[k, g][:].rearrange("r (u p e) -> r u p e", u=2, e=2),
                 in0=bank[:].rearrange("r (p u e) -> r u p e", u=2, e=2),
-                in1=spread["curv", j, g].rearrange("r (p u e) -> r u p e", u=2, e=2),
+                in1=spread["curv", chunk][:, half * KP : (half + 1) * KP].rearrange("r (u p e) -> r u p e", u=2, e=2),
                 op=MULT,
             )
 
         def ridge_term(k, c):
             v_ridge[k, c] = rotating("v_ridge", [P, KP], F32, RIDGE_AHEAD)
             nc.gpsimd.tensor_tensor(
-                out=v_ridge[k, c][:], in0=v_rows[k, c], in1=spread["ridge", k // PER_SITE, c], op=MULT
+                out=v_ridge[k, c][:], in0=v_rows[k, c], in1=spread["ridge", k // PER_SITE][:, c * KP : (c + 1) * KP], op=MULT
             )
 
         def stage_two(k, c):
@@ -215,50 +233,55 @@ def tile_logistic_hessian_vector_sites_k7_kernel(
             dst = out_1[g0 : g0 + groups, :, m, :].rearrange("g p m t -> p g (m t)")
             nc.sync.dma_start(out=dst.bitcast(I32), in_=codes[:].bitcast(I32))
 
-        def load_site(j):
-            load_scales(nc.sync, a_scale, a_scales, j, GD)
-            load_a(j, 0, KP)
-            load_v(2 * j + 1, 0, GD)
-            load_a(j, KP, NS - KP)
-            load_spread("curv", curv, j, 0, GS)
-            load_spread("ridge", ridge, j, 0, GD)
+        def load_between(j):
             load_scales(nc.sync, b_scale, b_scales, j, GS)
+            if j + 1 < SITES:
+                load_scales(nc.sync, a_scale, a_scales, j + 1, GD)
             load_b(j)
             if j + 1 < SITES:
-                load_v(2 * j + 2, 0, GD)
+                load_a(j + 1, 0, KP)
+                load_v(2 * j + 3, 0, GD)
+                load_a(j + 1, KP, NS - KP)
+            if j + 2 < SITES:
+                load_v(2 * j + 4, 0, GD)
 
         def stepped_blocks(rows):
             words = rows.bitcast(F32)
             return [words[:, u::2] for u in range(2)]
 
+        nc.vector.memset(factor_rows[:], 0.0)
         for j in range(SITES):
             clear_scales(a_scale, "a_scale", j, GD, NS)
             clear_scales(b_scale, "b_scale", j, GS, D)
+        load_rows(curv, 0, 24, 0)
+        load_rows(ridge, 0, 16, 32)
         load_v(0, 0, GD)
-        load_v(1, 0, GD)
-        load_scales(nc.sync, a_scale, a_scales, 0, GD)
         load_a(0, 0, KP)
-        load_spread("curv", curv, 0, 0, 1)
+        load_scales(nc.sync, a_scale, a_scales, 0, GD)
+        load_v(1, 0, GD)
         load_a(0, KP, KP)
-        load_spread("ridge", ridge, 0, 0, GD)
         load_a(0, 2 * KP, KP)
-        load_spread("curv", curv, 0, 1, GS - 1)
         load_v(2, 0, GD)
-        load_scales(nc.sync, b_scale, b_scales, 0, GS)
-        load_b(0)
-        for j in range(1, SITES):
-            load_site(j)
+        for j in range(SITES):
+            load_between(j)
 
         v_q[0] = []
-        for g in range(GD):
-            bank_v = turn(stepped_blocks(v_rows[0, g]), 2)
-            v_q[0].extend(quantize("v_half", copy_turned("v_half_turned", bank_v, 1, 2), 1, 2))
-        bank_v = turn(stepped_blocks(v_rows[1, 0]) + stepped_blocks(v_rows[1, 1]), 4)
-        v_q[1] = quantize("v", copy_turned("v_turned", bank_v, GD, 2), GD, 2)
-        for g in range(GS):
-            stage_one(0, g)
+        banks_v = [turn(stepped_blocks(v_rows[0, g]), 2) for g in range(GD)]
+        bank_c = turn(word_blocks(factor_rows, 1), 1)
+        v_q[0].extend(quantize("v_half", copy_turned("v_half_turned", banks_v[0], 1, 2), 1, 2))
+        nc.scalar.copy(out=columns[:], in_=bank_c[:, :64])
+        v_q[0].extend(quantize("v_half", copy_turned("v_half_turned", banks_v[1], 1, 2), 1, 2))
+        copy_spread("curv", 0, turn_columns("curv", 0))
+        sort_v(1, nc.vector.tensor_copy)
+        stage_one(0, 0)
+        v_q[1] = quantize("v", copy_turned("v_turned", turn(word_blocks(v_sorted[1], 4), 4), GD, 2), GD, 2)
+        for name, c in (("ridge", 0), ("curv", 1)):
+            copy_spread(name, c, turn_columns(name, c))
+        stage_one(0, 1)
+        stage_one(0, 2)
         for n in range(RIDGE_AHEAD):
             ridge_term(n // GD, n % GD)
+        to_spread = {1: [("ridge", 1), ("curv", 2)], 2: [("curv", 3)], 3: [("ridge", 2), ("curv", 4)], 4: [("curv", 5)], 5: [("ridge", 3)]}
 
         def turn_h(k):
             bank_h = turn(word_blocks(h_sorted[k, 0], 2) + word_blocks(h_sorted[k, 1], 2), 4)
@@ -278,7 +301,7 @@ def tile_logistic_hessian_vector_sites_k7_kernel(
                 round_y(old, 1)
                 store_y(old, 0, GD)
             if k == 1:
-                sort_v(2)
+                sort_v(2, nc.scalar.copy)
             for g in range(GS):
                 stage_one(k, g)
             if old >= 1:
@@ -291,6 +314,7 @@ def tile_logistic_hessian_vector_sites_k7_kernel(
             if old >= 0:
                 bank_y = turn_y(old, 0, GD)
             banks_h = turn_h(k)
+            banks_s = [turn_columns(name, c) for name, c in to_spread.get(k, [])]
 
             if k == 1:
                 h_q[0] = []
@@ -303,8 +327,10 @@ def tile_logistic_hessian_vector_sites_k7_kernel(
             quantize_h(k, *banks_h)
             if 0 <= old < UNITS - 3:
                 y_turned = copy_turned("y_turned", bank_y, GD, 2)
+            for (name, c), bank in zip(to_spread.get(k, []), banks_s):
+                copy_spread(name, c, bank)
             if k + 2 < UNITS:
-                sort_v(k + 2)
+                sort_v(k + 2, nc.scalar.copy)
 
         old, last = UNITS - 2, UNITS - 1
         stage_two(old, 0)

from contextlib import ExitStack

import concourse.mybir as mybir
from concourse.masks import make_identity

SITES, R, NS, D = 4, 256, 1536, 1024
FLOPS = 2 * 2 * SITES * R * NS * D

F32 = mybir.dt.float32
BF16 = mybir.dt.bfloat16
I32 = mybir.dt.int32
U32 = mybir.dt.uint32
U8 = mybir.dt.uint8
FP8X4 = mybir.dt.float8_e4m3fn_x4
FP4X4 = mybir.dt.float4_e2m1fn_x4
MULT = mybir.AluOpType.mult
ADD = mybir.AluOpType.add

P = 128
KP = 512
GD = D // KP
GS = NS // KP
UNITS = SITES * R // P
PER_SITE = R // P
BANKS = 8
RIDGE_AHEAD = 3
CHUNK = 1024
FIRST_ROW = {"curv": 0, "ridge": 32}


def tile_logistic_hessian_vector_sites_k7_kernel(
    tc, v, a_words, a_scales, curv, b_words, b_scales, ridge, out_0, out_1, out_2
):
    nc = tc.nc
    with ExitStack() as ctx:
        keep = ctx.enter_context(tc.tile_pool(name="keep", bufs=1))
        work = ctx.enter_context(tc.tile_pool(name="work", bufs=2))
        psum = ctx.enter_context(tc.psum_pool(name="psum", bufs=1))

        ident = keep.tile([P, P], F32, name="ident")
        make_identity(nc, ident[:])
        ctx.enter_context(tc.manual_schedule())

        taken = []

        def next_bank():
            name = "bank%d" % (len(taken) % BANKS)
            bank = psum.tile([P, KP], F32, name=name, tag=name)
            taken.append(name)
            return bank

        def kept(name, shape, dtype):
            tile = keep.tile(shape, dtype, name=name, tag=name, align_bytes=64)
            return tile

        def rotating(name, shape, dtype, bufs):
            tile = work.tile(shape, dtype, name=name, tag=name, bufs=bufs, align_bytes=64)
            return tile

        a_scale, b_scale, a_parts, b_code, v_rows = {}, {}, {}, {}, {}
        spread, v_tile = {}, {}
        factor_rows = kept("factor_rows", [P, 2 * P], BF16)
        columns = kept("columns", [P, 64], F32)
        v_sorted, v_q, h_sorted, h_turned, h_q, v_ridge, y_rows, y_sorted = {}, {}, {}, {}, {}, {}, {}, {}
        y_scale = kept("y_scale", [P, GD, SITES * R], U8)

        def clear_scales(store, name, j, groups, width):
            store[j] = kept("%s%d" % (name, j), [P, groups, width], U8)
            nc.vector.memset(store[j][:].rearrange("p g n -> p (g n)").bitcast(I32), 0)

        def load_scales(queue, store, dram, j, groups):
            for r in range(4):
                rows = dram[groups * j : groups * (j + 1), r:16:4, :].rearrange("g q n -> q g n")
                queue.dma_start(out=store[j][r:P:32, :, :].bitcast(I32), in_=rows.bitcast(I32))

        def load_a(j, n0, width):
            part = kept("a%d_%d" % (j, n0), [P, GD, 2 * width], U8)
            src = a_words[GD * j : GD * (j + 1), :, 2 * n0 : 2 * (n0 + width)].rearrange("g p n -> p g n")
            nc.sync.dma_start(out=part[:].bitcast(I32), in_=src.bitcast(I32))
            for n in range(n0, n0 + width, KP):
                a_parts[j, n // KP] = (part, n - n0)

        def load_b(j):
            b_code[j] = kept("b%d" % j, [P, GS, 2 * D], U8)
            src = b_words[GS * j : GS * (j + 1), :, :].rearrange("g p n -> p g n")
            nc.sync.dma_start(out=b_code[j][:].bitcast(I32), in_=src.bitcast(I32))

        def load_v(k, g0, groups):
            j, h = divmod(k, PER_SITE)
            tile = kept("v%d_%d" % (k, g0), [P, groups * KP], BF16)
            nc.sync.dma_start(out=tile[:], in_=v[j, h * P : (h + 1) * P, g0 * KP : (g0 + groups) * KP])
            for g in range(groups):
                v_rows[k, g0 + g] = tile[:, g * KP : (g + 1) * KP]
            v_tile[k] = tile

        def load_rows(dram, r0, count, p0):
            flat = dram.rearrange("j n -> (j n)")[r0 * 2 * P : (r0 + count) * 2 * P]
            nc.scalar.dma_start(out=factor_rows[p0 : p0 + count, :], in_=flat.rearrange("(r n) -> r n", n=2 * P))

        def turn(words, count):
            bank = next_bank()
            for i in range(count):
                nc.tensor.transpose(bank[:, i * P : (i + 1) * P], words[i], ident[:])
            return bank

        def word_blocks(tile, count):
            words = tile[:].bitcast(F32)
            return [words[:, i * P : (i + 1) * P] for i in range(count)]

        def turn_columns(name, c):
            first = FIRST_ROW[name] + 4 * c
            return turn([columns[:, i : i + 1].to_broadcast([P, P]) for i in range(first, first + 4)], 4)

        def copy_spread(name, c, bank):
            spread[name, c] = kept("%s_spread%d" % (name, c), [P, CHUNK], BF16)
            words = spread[name, c][:].bitcast(F32)
            if name == "curv":
                nc.scalar.copy(
                    out=words.rearrange("m (g u p) -> m g u p", g=2, u=2),
                    in_=bank[:].rearrange("m (g p u) -> m g u p", g=2, u=2),
                )
            else:
                nc.scalar.copy(out=words, in_=bank[:])

        def copy_turned(name, bank, groups, bufs):
            tile = rotating(name, [P, groups * KP], BF16, bufs)
            nc.scalar.copy(
                out=tile[:].bitcast(F32).rearrange("p (g r u) -> p g r u", g=groups, u=2),
                in_=bank[:, : groups * 2 * P].rearrange("p (g u r) -> p g r u", g=groups, u=2),
            )
            return tile

        def quantize(name, tile, groups, bufs):
            codes = rotating(name + "_codes", [P, groups * P], U32, bufs)
            scales = rotating(name + "_scales", [P, groups * P], U8, bufs)
            nc.vector.quantize_mx(out=codes[:].bitcast(FP8X4), scales=scales[:], in_=tile[:])
            return [(codes[:, g * P : (g + 1) * P], scales[:, g * P : (g + 1) * P]) for g in range(groups)]

        def sort_v(k, copy):
            v_sorted[k] = rotating("v_sorted", [P, D], BF16, 2)
            copy(
                out=v_sorted[k][:].bitcast(F32).rearrange("r (g u p) -> r g u p", g=GD, u=2),
                in_=v_tile[k][:].bitcast(F32).rearrange("r (g p u) -> r g u p", g=GD, u=2),
            )

        def stage_one(k, g):
            j = k // PER_SITE
            part, n0 = a_parts[j, g]
            bank = next_bank()
            for c in range(GD):
                codes, scales = v_q[k][c]
                nc.tensor.matmul_mx(
                    out=bank[:],
                    lhsT=codes.bitcast(FP8X4),
                    lhsT_scale=scales,
                    rhs=part[:, c, 2 * n0 : 2 * (n0 + KP)].bitcast(FP4X4),
                    rhs_scale=a_scale[j][:, c, g * KP : (g + 1) * KP],
                    start=(c == 0),
                    stop=(c == GD - 1),
                )
            chunk, half = divmod(GS * j + g, 2)
            h_sorted[k, g] = rotating("h_sorted%d" % g, [P, KP], BF16, 2)
            nc.vector.tensor_tensor(
                out=h_sorted[k, g][:].rearrange("r (u p e) -> r u p e", u=2, e=2),
                in0=bank[:].rearrange("r (p u e) -> r u p e", u=2, e=2),
                in1=spread["curv", chunk][:, half * KP : (half + 1) * KP].rearrange("r (u p e) -> r u p e", u=2, e=2),
                op=MULT,
            )

        def ridge_term(k, c):
            v_ridge[k, c] = rotating("v_ridge", [P, KP], F32, RIDGE_AHEAD)
            nc.gpsimd.tensor_tensor(
                out=v_ridge[k, c][:], in0=v_rows[k, c], in1=spread["ridge", k // PER_SITE][:, c * KP : (c + 1) * KP], op=MULT
            )

        def stage_two(k, c):
            j = k // PER_SITE
            cols = slice(c * KP, (c + 1) * KP)
            bank = next_bank()
            for g in range(GS):
                codes, scales = h_q[k][g]
                nc.tensor.matmul_mx(
                    out=bank[:],
                    lhsT=codes.bitcast(FP8X4),
                    lhsT_scale=scales,
                    rhs=b_code[j][:, g, 2 * c * KP : 2 * (c + 1) * KP].bitcast(FP4X4),
                    rhs_scale=b_scale[j][:, g, cols],
                    start=(g == 0),
                    stop=(g == GS - 1),
                )
            if c == 0:
                y_rows[k] = kept("y%d" % k, [P, D], F32)
            if (k, c) == (UNITS - 1, GD - 1):
                y_sorted[k, c] = rotating("y_sorted%d" % c, [P, KP], BF16, 2)
                nc.vector.tensor_tensor(
                    out=y_sorted[k, c][:].rearrange("r (u p e) -> r u p e", u=2, e=2),
                    in0=bank[:].rearrange("r (p u e) -> r u p e", u=2, e=2),
                    in1=v_ridge[k, c][:].rearrange("r (p u e) -> r u p e", u=2, e=2),
                    op=ADD,
                )
            nc.vector.tensor_tensor(out=y_rows[k][:, cols], in0=bank[:], in1=v_ridge[k, c][:], op=ADD)
            ahead = GD * k + c + RIDGE_AHEAD
            if ahead < GD * UNITS:
                ridge_term(ahead // GD, ahead % GD)

        def round_y(k, c):
            y_sorted[k, c] = rotating("y_sorted%d" % c, [P, KP], BF16, 2)
            nc.scalar.copy(
                out=y_sorted[k, c][:].rearrange("r (u p e) -> r u p e", u=2, e=2),
                in_=y_rows[k][:, c * KP : (c + 1) * KP].rearrange("r (p u e) -> r u p e", u=2, e=2),
            )

        def store_y(k, c0, count):
            j, h = divmod(k, PER_SITE)
            cols = slice(c0 * KP, (c0 + count) * KP)
            nc.sync.dma_start(out=out_0[j, h * P : (h + 1) * P, cols], in_=y_rows[k][:, cols])

        def turn_y(k, g0, groups):
            blocks = []
            for g in range(g0, g0 + groups):
                blocks.extend(word_blocks(y_sorted[k, g], 2))
            return turn(blocks, 2 * groups)

        def planes(k, g0, groups, tile):
            m = slice(k * P, (k + 1) * P)
            codes = kept("y_codes%d_%d" % (k, g0), [P, groups, P], U32)
            for g in range(groups):
                nc.vector.quantize_mx(
                    out=codes[:, g, :].bitcast(FP8X4),
                    scales=y_scale[:, g0 + g, m],
                    in_=tile[:, g * KP : (g + 1) * KP],
                )
            dst = out_1[g0 : g0 + groups, :, m, :].rearrange("g p m t -> p g (m t)")
            nc.sync.dma_start(out=dst.bitcast(I32), in_=codes[:].bitcast(I32))

        def load_between(j):
            load_scales(nc.sync, b_scale, b_scales, j, GS)
            if j + 1 < SITES:
                load_scales(nc.sync, a_scale, a_scales, j + 1, GD)
            load_b(j)
            if j + 1 < SITES:
                load_a(j + 1, 0, KP)
                load_v(2 * j + 3, 0, GD)
                load_a(j + 1, KP, NS - KP)
            if j + 2 < SITES:
                load_v(2 * j + 4, 0, GD)

        def stepped_blocks(rows):
            words = rows.bitcast(F32)
            return [words[:, u::2] for u in range(2)]

        nc.vector.memset(factor_rows[:], 0.0)
        for j in range(SITES):
            clear_scales(a_scale, "a_scale", j, GD, NS)
            clear_scales(b_scale, "b_scale", j, GS, D)
        load_rows(curv, 0, 24, 0)
        load_rows(ridge, 0, 16, 32)
        load_v(0, 0, GD)
        load_a(0, 0, KP)
        load_scales(nc.sync, a_scale, a_scales, 0, GD)
        load_v(1, 0, GD)
        load_a(0, KP, KP)
        load_a(0, 2 * KP, KP)
        load_v(2, 0, GD)
        for j in range(SITES):
            load_between(j)

        v_q[0] = []
        banks_v = [turn(stepped_blocks(v_rows[0, g]), 2) for g in range(GD)]
        bank_c = turn(word_blocks(factor_rows, 1), 1)
        v_q[0].extend(quantize("v_half", copy_turned("v_half_turned", banks_v[0], 1, 2), 1, 2))
        nc.scalar.copy(out=columns[:], in_=bank_c[:, :64])
        v_q[0].extend(quantize("v_half", copy_turned("v_half_turned", banks_v[1], 1, 2), 1, 2))
        copy_spread("curv", 0, turn_columns("curv", 0))
        sort_v(1, nc.vector.tensor_copy)
        stage_one(0, 0)
        v_q[1] = quantize("v", copy_turned("v_turned", turn(word_blocks(v_sorted[1], 4), 4), GD, 2), GD, 2)
        for name, c in (("ridge", 0), ("curv", 1)):
            copy_spread(name, c, turn_columns(name, c))
        stage_one(0, 1)
        stage_one(0, 2)
        for n in range(RIDGE_AHEAD):
            ridge_term(n // GD, n % GD)
        to_spread = {1: [("ridge", 1), ("curv", 2)], 2: [("curv", 3)], 3: [("ridge", 2), ("curv", 4)], 4: [("curv", 5)], 5: [("ridge", 3)]}

        def turn_h(k):
            bank_h = turn(word_blocks(h_sorted[k, 0], 2) + word_blocks(h_sorted[k, 1], 2), 4)
            bank_last = turn(word_blocks(h_sorted[k, 2], 2), 2)
            return bank_h, bank_last

        def quantize_h(k, bank_h, bank_last):
            h_q[k] = quantize("h", copy_turned("h_turned", bank_h, 2, 2), 2, 3)
            h_q[k].extend(quantize("h_last", copy_turned("h_last_turned", bank_last, 1, 2), 1, 3))

        for k in range(1, UNITS):
            old = k - 2
            if old >= 0:
                stage_two(old, 0)
                round_y(old, 0)
                stage_two(old, 1)
                round_y(old, 1)
                store_y(old, 0, GD)
            if k == 1:
                sort_v(2, nc.scalar.copy)
            for g in range(GS):
                stage_one(k, g)
            if old >= 1:
                planes(old - 1, 0, GD, y_turned)

            if k == 1:
                banks_first = [turn(word_blocks(h_sorted[0, g], 2), 2) for g in range(GS)]
            if k + 1 < UNITS:
                bank_v = turn(word_blocks(v_sorted[k + 1], 4), 4)
            if old >= 0:
                bank_y = turn_y(old, 0, GD)
            banks_h = turn_h(k)
            banks_s = [turn_columns(name, c) for name, c in to_spread.get(k, [])]

            if k == 1:
                h_q[0] = []
                for bank in banks_first:
                    h_q[0].extend(quantize("h_first", copy_turned("h_first_turned", bank, 1, GS), 1, GS))
            if k + 1 < UNITS:
                v_q[k + 1] = quantize("v", copy_turned("v_turned", bank_v, GD, 2), GD, 2)
            else:
                planes(old, 0, GD, copy_turned("y_turned", bank_y, GD, 2))
            quantize_h(k, *banks_h)
            if 0 <= old < UNITS - 3:
                y_turned = copy_turned("y_turned", bank_y, GD, 2)
            for (name, c), bank in zip(to_spread.get(k, []), banks_s):
                copy_spread(name, c, bank)
            if k + 2 < UNITS:
                sort_v(k + 2, nc.scalar.copy)

        old, last = UNITS - 2, UNITS - 1
        stage_two(old, 0)
        round_y(old, 0)
        stage_two(old, 1)
        round_y(old, 1)
        store_y(old, 0, GD)
        stage_two(last, 0)
        round_y(last, 0)
        store_y(last, 0, 1)
        stage_two(last, 1)
        bank_y = turn_y(old, 0, GD)
        bank_first = turn_y(last, 0, 1)
        bank_second = turn_y(last, 1, 1)
        store_y(last, 1, 1)
        planes(old, 0, GD, copy_turned("y_turned", bank_y, GD, 2))
        planes(last, 0, 1, copy_turned("y_half_turned", bank_first, 1, 2))
        planes(last, 1, 1, copy_turned("y_half_turned", bank_second, 1, 2))
        for q in range(4):
            queue = nc.scalar if q % 2 else nc.sync
            dst = out_2[:, 4 * q : 4 * q + 4, :].rearrange("g q m -> q g m")
            queue.dma_start(out=dst.bitcast(I32), in_=y_scale[32 * q : 32 * q + 4, :, :].bitcast(I32))
